import numpy as np, ml_dtypes
CORES = [2,10,18,26,34,42,50,58,66,74,82,90,98,106,114,122,130,138,146,154,162,170,178,186,194,202,210,218,226,234,242,250]
N = 32
ROOT = 17
def setup_inputs(rng):
    return {"x": rng.standard_normal((N, 128, 256), dtype=np.float32).astype(ml_dtypes.bfloat16)}
def reference(x):
    y = np.full(x.shape, np.nan, x.dtype)
    y[ROOT] = x.max(axis=0)
    return {"y": y}

from concourse.bass import DstId, RemoteDMATransfer

P = 16
W = 16
ROOT_CORE = 138

SCRATCH = {
    "xs": ("dram", [P, 128, W], "bfloat16"),
    "gl": ("dram", [32, 128, W], "bfloat16"),
    "res": ("dram", [P, 128, W], "bfloat16"),
}
SEMAPHORES = ["loaded", "sent", "arrived", "done", "stored"]


def gatherer(q):
    c = (q // 8) * 128 + (2 * (q % 8) + 1) * 8 + 2
    return c + 1 if c == ROOT_CORE else c


def rank_program(g, core, T, topo):
    rank = T.rank_of(core)
    gath = [gatherer(q) for q in range(P)]
    mine = gath.index(core) if core in gath else None
    if rank is None and mine is None:
        return
    sent = 0

    if rank is not None:
        g.sync.dma_start(T.xs[:], T.x[:]).then_inc(T.sem.loaded, 16)
        g.wait_ge(T.sem.loaded, 16)
        pair = (rank // 16) * 8 + (rank % 16) // 2
        order = [(pair + 1 + i) % P for i in range(P)]
        order = [q for q in order if gath[q] != core]
        for lo in range(0, len(order), 8):
            trs = []
            for i, q in enumerate(order[lo:lo + 8]):
                rid, pid = topo.addr(gath[q], core)
                trs.append(RemoteDMATransfer(dst_ids=[DstId(rid=rid, pnc=pid)], dma_engine_mask=1 << i,
                                             remote_sem=T.sem.arrived, src=T.xs[q], dst=T.gl[rank]))
                sent += 1
            g.remote_dma_fused(trs, local_sem=T.sem.sent)

    if mine is not None:
        srcs = [T.xs[mine] if r == rank else T.gl[r] for r in range(32)]
        g.wait_ge(T.sem.arrived, 32 if rank is None else 31)
        rid, pid = topo.addr(ROOT_CORE, core)
        m = topo.mask(core, ROOT_CORE)
        g.remote_dma_fused([RemoteDMATransfer(dst_ids=[DstId(rid=rid, pnc=pid)], dma_engine_mask=m,
                                              remote_sem=T.sem.done, srcs=srcs, dsts=[T.res[mine]], alu_op=2)],
                           local_sem=T.sem.sent)
        sent += 16 if m == 0xFFFF else 8

    if core == ROOT_CORE:
        g.sync.wait_ge(T.sem.done, 15 * 8 + 16)
        g.sync.dma_start(T.y[:], T.res[:]).then_inc(T.sem.stored, 16)
        g.sync.wait_ge(T.sem.stored, 16)

    g.wait_ge(T.sem.sent, sent)
